import numpy as np
import ml_dtypes

BF16 = ml_dtypes.bfloat16


def bf(x):
    return np.asarray(x, np.float32).astype(BF16)


def f32(x):
    return np.asarray(x, np.float32)


def f64(x):
    return np.asarray(x).astype(np.float64)


def striped(idx):
    return np.tile(idx.reshape(-1, 16).T, (8, 1))


S, K, M, N = 2048, 256, 256, 768


def setup_inputs():
    return {"table": bf(np.random.standard_normal((K, S))), "w": bf(np.random.standard_normal((K, M)) / np.sqrt(K)), "b": f32(0.5 * np.random.standard_normal((M, 1))), "offs": striped(np.random.permutation(S)[:N])}


def reference(table, w, b, offs):
    idx = offs[:16].T.reshape(-1)
    x = f64(table)[:, idx]
    y = f64(w).T @ x
    return y + f64(b)

@@ -1,0 +1,51 @@
+import concourse.mybir as mybir
+
+BF16, F32, U16 = mybir.dt.bfloat16, mybir.dt.float32, mybir.dt.uint16
+
+P = 128
+S = 2048
+K = 256
+M = 256
+N = 768
+PIECE = 384
+K_BLOCKS, M_BLOCKS, PIECES = K // P, M // P, N // PIECE
+
+FLOPS = 2 * K * M * N
+
+
+def tile_gather_matmul_kernel(tc, table, w, b, offs, out):
+    nc = tc.nc
+    with (
+        tc.tile_pool(name="held", bufs=1) as held,
+        tc.tile_pool(name="staged", bufs=2) as staged,
+        tc.psum_pool(name="psum", bufs=2) as psum,
+    ):
+        offsets = held.tile([P, N // 16], U16, name="offsets")
+        nc.sync.dma_start(offsets[:], offs)
+
+        windows = [held.tile([P, S], BF16, name=f"window{kb}") for kb in range(K_BLOCKS)]
+        for kb in range(K_BLOCKS):
+            nc.sync.dma_start(windows[kb][:], table[kb * P : (kb + 1) * P, :])
+
+        weights = held.tile([P, K_BLOCKS, M], BF16, name="weights")
+        nc.scalar.dma_start(weights[:], w.rearrange("(kb p) m -> p kb m", p=P))
+        bias = held.tile([P, M_BLOCKS], F32, name="bias")
+        nc.scalar.dma_start(bias[:], b.rearrange("(mb p) o -> p (mb o)", p=P))
+
+        for mb in range(M_BLOCKS):
+            for piece in range(PIECES):
+                entries = offsets[:, piece * (PIECE // 16) : (piece + 1) * (PIECE // 16)]
+                product = psum.tile([P, PIECE], F32, name="product")
+                for kb in range(K_BLOCKS):
+                    nc.tensor.matmul(
+                        product[:],
+                        weights[:, kb, mb * P : (mb + 1) * P],
+                        windows[kb][:].indirect(entries),
+                        start=(kb == 0),
+                        stop=(kb == K_BLOCKS - 1),
+                    )
+                biased = staged.tile([P, PIECE], F32, name="biased")
+                nc.vector.tensor_scalar_add(biased[:], product[:], bias[:, mb : mb + 1])
+                nc.sync.dma_start(
+                    out[mb * P : (mb + 1) * P, piece * PIECE : (piece + 1) * PIECE], biased[:]
+                )

@@ -1,14 +1,15 @@
 import concourse.mybir as mybir
 
 BF16, F32, U16 = mybir.dt.bfloat16, mybir.dt.float32, mybir.dt.uint16
+IDENTITY = mybir.ActivationFunctionType.Identity
 
 P = 128
 S = 2048
 K = 256
 M = 256
 N = 768
-PIECE = 384
-K_BLOCKS, M_BLOCKS, PIECES = K // P, M // P, N // PIECE
+K_BLOCKS, M_BLOCKS = K // P, M // P
+PIECES = ((0, 512), (512, 256))
 
 FLOPS = 2 * K * M * N
 
@@ -17,8 +18,7 @@ def tile_gather_matmul_kernel(tc, table, w, b, offs, out):
     nc = tc.nc
     with (
         tc.tile_pool(name="held", bufs=1) as held,
-        tc.tile_pool(name="staged", bufs=2) as staged,
-        tc.psum_pool(name="psum", bufs=2) as psum,
+        tc.psum_pool(name="psum", bufs=1) as psum,
     ):
         offsets = held.tile([P, N // 16], U16, name="offsets")
         nc.sync.dma_start(offsets[:], offs)
@@ -32,11 +32,18 @@ def tile_gather_matmul_kernel(tc, table, w, b, offs, out):
         bias = held.tile([P, M_BLOCKS], F32, name="bias")
         nc.scalar.dma_start(bias[:], b.rearrange("(mb p) o -> p (mb o)", p=P))
 
-        for mb in range(M_BLOCKS):
-            for piece in range(PIECES):
-                entries = offsets[:, piece * (PIECE // 16) : (piece + 1) * (PIECE // 16)]
-                product = psum.tile([P, PIECE], F32, name="product")
-                for kb in range(K_BLOCKS):
+        products = {
+            (mb, first): psum.tile([P, count], F32, name=f"product_{mb}_{first}")
+            for first, count in PIECES
+            for mb in range(M_BLOCKS)
+        }
+        store_queues = (nc.sync, nc.scalar)
+
+        for kb in range(K_BLOCKS):
+            for first, count in PIECES:
+                entries = offsets[:, first // 16 : (first + count) // 16]
+                for mb in range(M_BLOCKS):
+                    product = products[(mb, first)]
                     nc.tensor.matmul(
                         product[:],
                         weights[:, kb, mb * P : (mb + 1) * P],
@@ -44,8 +51,12 @@ def tile_gather_matmul_kernel(tc, table, w, b, offs, out):
                         start=(kb == 0),
                         stop=(kb == K_BLOCKS - 1),
                     )
-                biased = staged.tile([P, PIECE], F32, name="biased")
-                nc.vector.tensor_scalar_add(biased[:], product[:], bias[:, mb : mb + 1])
-                nc.sync.dma_start(
-                    out[mb * P : (mb + 1) * P, piece * PIECE : (piece + 1) * PIECE], biased[:]
-                )
+                    if kb == K_BLOCKS - 1:
+                        biased = held.tile([P, count], F32, name=f"biased_{mb}_{first}")
+                        if mb == 0:
+                            nc.vector.tensor_scalar_add(biased[:], product[:], bias[:, mb : mb + 1])
+                        else:
+                            nc.scalar.activation(biased[:], product[:], IDENTITY, bias=bias[:, mb : mb + 1])
+                        store_queues[mb].dma_start(
+                            out[mb * P : (mb + 1) * P, first : first + count], biased[:]
+                        )

@@ -10,6 +10,8 @@ M = 256
 N = 768
 K_BLOCKS, M_BLOCKS = K // P, M // P
 PIECES = ((0, 512), (512, 256))
+BANK = 512
+WARM_UPS = 5
 
 FLOPS = 2 * K * M * N
 
@@ -31,6 +33,12 @@ def tile_gather_matmul_kernel(tc, table, w, b, offs, out):
         nc.scalar.dma_start(weights[:], w.rearrange("(kb p) m -> p kb m", p=P))
         bias = held.tile([P, M_BLOCKS], F32, name="bias")
         nc.scalar.dma_start(bias[:], b.rearrange("(mb p) o -> p (mb o)", p=P))
+
+        zeros = held.tile([P, BANK], BF16, name="zeros")
+        nc.vector.memset(zeros[:], 0.0)
+        unread = psum.tile([P, BANK], F32, name="unread")
+        for warm_up in range(WARM_UPS):
+            nc.tensor.matmul(unread[:], zeros[:, 0:P], zeros[:], start=True, stop=True)
 
         products = {
             (mb, first): psum.tile([P, count], F32, name=f"product_{mb}_{first}")

@@ -10,8 +10,6 @@ M = 256
 N = 768
 K_BLOCKS, M_BLOCKS = K // P, M // P
 PIECES = ((0, 512), (512, 256))
-BANK = 512
-WARM_UPS = 5
 
 FLOPS = 2 * K * M * N
 
@@ -25,20 +23,21 @@ def tile_gather_matmul_kernel(tc, table, w, b, offs, out):
         offsets = held.tile([P, N // 16], U16, name="offsets")
         nc.sync.dma_start(offsets[:], offs)
 
-        windows = [held.tile([P, S], BF16, name=f"window{kb}") for kb in range(K_BLOCKS)]
-        for kb in range(K_BLOCKS):
-            nc.sync.dma_start(windows[kb][:], table[kb * P : (kb + 1) * P, :])
-
         weights = held.tile([P, K_BLOCKS, M], BF16, name="weights")
         nc.scalar.dma_start(weights[:], w.rearrange("(kb p) m -> p kb m", p=P))
-        bias = held.tile([P, M_BLOCKS], F32, name="bias")
-        nc.scalar.dma_start(bias[:], b.rearrange("(mb p) o -> p (mb o)", p=P))
 
-        zeros = held.tile([P, BANK], BF16, name="zeros")
-        nc.vector.memset(zeros[:], 0.0)
-        unread = psum.tile([P, BANK], F32, name="unread")
-        for warm_up in range(WARM_UPS):
-            nc.tensor.matmul(unread[:], zeros[:, 0:P], zeros[:], start=True, stop=True)
+        windows = [held.tile([P, S], BF16, name=f"window{kb}") for kb in range(K_BLOCKS)]
+        load_queues = (nc.sync, nc.scalar)
+        run = S // 4
+        for kb in range(K_BLOCKS):
+            for c in range(4):
+                load_queues[c % 2].dma_start(
+                    windows[kb][:, c * run : (c + 1) * run],
+                    table[kb * P : (kb + 1) * P, c * run : (c + 1) * run],
+                )
+
+        bias = held.tile([P, M_BLOCKS], F32, name="bias")
+        nc.sync.dma_start(bias[:], b.rearrange("(mb p) o -> p (mb o)", p=P))
 
         products = {
             (mb, first): psum.tile([P, count], F32, name=f"product_{mb}_{first}")

@@ -1,7 +1,6 @@
 import concourse.mybir as mybir
 
 BF16, F32, U16 = mybir.dt.bfloat16, mybir.dt.float32, mybir.dt.uint16
-IDENTITY = mybir.ActivationFunctionType.Identity
 
 P = 128
 S = 2048
@@ -10,6 +9,7 @@ M = 256
 N = 768
 K_BLOCKS, M_BLOCKS = K // P, M // P
 PIECES = ((0, 512), (512, 256))
+RUNS = 4
 
 FLOPS = 2 * K * M * N
 
@@ -27,43 +27,29 @@ def tile_gather_matmul_kernel(tc, table, w, b, offs, out):
         nc.scalar.dma_start(weights[:], w.rearrange("(kb p) m -> p kb m", p=P))
 
         windows = [held.tile([P, S], BF16, name=f"window{kb}") for kb in range(K_BLOCKS)]
-        load_queues = (nc.sync, nc.scalar)
-        run = S // 4
+        queues = (nc.sync, nc.scalar)
         for kb in range(K_BLOCKS):
-            for c in range(4):
-                load_queues[c % 2].dma_start(
-                    windows[kb][:, c * run : (c + 1) * run],
-                    table[kb * P : (kb + 1) * P, c * run : (c + 1) * run],
-                )
+            for r in range(RUNS):
+                columns = slice(r * (S // RUNS), (r + 1) * (S // RUNS))
+                queues[r % 2].dma_start(windows[kb][:, columns], table[kb * P : (kb + 1) * P, columns])
 
         bias = held.tile([P, M_BLOCKS], F32, name="bias")
         nc.sync.dma_start(bias[:], b.rearrange("(mb p) o -> p (mb o)", p=P))
 
-        products = {
-            (mb, first): psum.tile([P, count], F32, name=f"product_{mb}_{first}")
-            for first, count in PIECES
-            for mb in range(M_BLOCKS)
-        }
-        store_queues = (nc.sync, nc.scalar)
-
-        for kb in range(K_BLOCKS):
-            for first, count in PIECES:
-                entries = offsets[:, first // 16 : (first + count) // 16]
+        block_orders = ((0, 1), (1, 0))
+        for (first, count), block_order in zip(PIECES, block_orders):
+            entries = offsets[:, first // 16 : (first + count) // 16]
+            products = [psum.tile([P, count], F32, name=f"product_{mb}_{first}") for mb in range(M_BLOCKS)]
+            for kb in block_order:
                 for mb in range(M_BLOCKS):
-                    product = products[(mb, first)]
                     nc.tensor.matmul(
-                        product[:],
+                        products[mb][:],
                         weights[:, kb, mb * P : (mb + 1) * P],
                         windows[kb][:].indirect(entries),
-                        start=(kb == 0),
-                        stop=(kb == K_BLOCKS - 1),
+                        start=(kb == block_order[0]),
+                        stop=(kb == block_order[-1]),
                     )
-                    if kb == K_BLOCKS - 1:
-                        biased = held.tile([P, count], F32, name=f"biased_{mb}_{first}")
-                        if mb == 0:
-                            nc.vector.tensor_scalar_add(biased[:], product[:], bias[:, mb : mb + 1])
-                        else:
-                            nc.scalar.activation(biased[:], product[:], IDENTITY, bias=bias[:, mb : mb + 1])
-                        store_queues[mb].dma_start(
-                            out[mb * P : (mb + 1) * P, first : first + count], biased[:]
-                        )
+            for mb in range(M_BLOCKS):
+                biased = held.tile([P, count], F32, name=f"biased_{mb}_{first}")
+                nc.vector.tensor_scalar_add(biased[:], products[mb][:], bias[:, mb : mb + 1])
+                queues[mb].dma_start(out[mb * P : (mb + 1) * P, first : first + count], biased[:])

@@ -9,7 +9,7 @@ M = 256
 N = 768
 K_BLOCKS, M_BLOCKS = K // P, M // P
 PIECES = ((0, 512), (512, 256))
-RUNS = 4
+RUNS = 2
 
 FLOPS = 2 * K * M * N
 

@@ -9,7 +9,7 @@ M = 256
 N = 768
 K_BLOCKS, M_BLOCKS = K // P, M // P
 PIECES = ((0, 512), (512, 256))
-RUNS = 2
+QUEUES = 2
 
 FLOPS = 2 * K * M * N
 
@@ -29,9 +29,8 @@ def tile_gather_matmul_kernel(tc, table, w, b, offs, out):
         windows = [held.tile([P, S], BF16, name=f"window{kb}") for kb in range(K_BLOCKS)]
         queues = (nc.sync, nc.scalar)
         for kb in range(K_BLOCKS):
-            for r in range(RUNS):
-                columns = slice(r * (S // RUNS), (r + 1) * (S // RUNS))
-                queues[r % 2].dma_start(windows[kb][:, columns], table[kb * P : (kb + 1) * P, columns])
+            for q in range(QUEUES):
+                queues[q].dma_start(windows[kb][q::QUEUES, :], table[kb * P + q : (kb + 1) * P : QUEUES, :])
 
         bias = held.tile([P, M_BLOCKS], F32, name="bias")
         nc.sync.dma_start(bias[:], b.rearrange("(mb p) o -> p (mb o)", p=P))

@@ -51,4 +51,7 @@ def tile_gather_matmul_kernel(tc, table, w, b, offs, out):
             for mb in range(M_BLOCKS):
                 biased = held.tile([P, count], F32, name=f"biased_{mb}_{first}")
                 nc.vector.tensor_scalar_add(biased[:], products[mb][:], bias[:, mb : mb + 1])
-                queues[mb].dma_start(out[mb * P : (mb + 1) * P, first : first + count], biased[:])
+                for q in range(QUEUES):
+                    queues[q].dma_start(
+                        out[mb * P + q : (mb + 1) * P : QUEUES, first : first + count], biased[q::QUEUES, :]
+                    )

import concourse.mybir as mybir

BF16, F32, U16 = mybir.dt.bfloat16, mybir.dt.float32, mybir.dt.uint16

P = 128
S = 2048
K = 256
M = 256
N = 768
K_BLOCKS, M_BLOCKS = K // P, M // P
PIECES = ((0, 512), (512, 256))
QUEUES = 2

FLOPS = 2 * K * M * N


def tile_gather_matmul_kernel(tc, table, w, b, offs, out):
    nc = tc.nc
    with (
        tc.tile_pool(name="held", bufs=1) as held,
        tc.psum_pool(name="psum", bufs=1) as psum,
    ):
        offsets = held.tile([P, N // 16], U16, name="offsets")
        nc.sync.dma_start(offsets[:], offs)

        weights = held.tile([P, K_BLOCKS, M], BF16, name="weights")
        nc.scalar.dma_start(weights[:], w.rearrange("(kb p) m -> p kb m", p=P))

        windows = [held.tile([P, S], BF16, name=f"window{kb}") for kb in range(K_BLOCKS)]
        queues = (nc.sync, nc.scalar)
        for kb in range(K_BLOCKS):
            for q in range(QUEUES):
                queues[q].dma_start(windows[kb][q::QUEUES, :], table[kb * P + q : (kb + 1) * P : QUEUES, :])

        bias = held.tile([P, M_BLOCKS], F32, name="bias")
        nc.sync.dma_start(bias[:], b.rearrange("(mb p) o -> p (mb o)", p=P))

        block_orders = ((0, 1), (1, 0))
        for (first, count), block_order in zip(PIECES, block_orders):
            entries = offsets[:, first // 16 : (first + count) // 16]
            products = [psum.tile([P, count], F32, name=f"product_{mb}_{first}") for mb in range(M_BLOCKS)]
            for kb in block_order:
                for mb in range(M_BLOCKS):
                    nc.tensor.matmul(
                        products[mb][:],
                        weights[:, kb, mb * P : (mb + 1) * P],
                        windows[kb][:].indirect(entries),
                        start=(kb == block_order[0]),
                        stop=(kb == block_order[-1]),
                    )
            for mb in range(M_BLOCKS):
                biased = held.tile([P, count], F32, name=f"biased_{mb}_{first}")
                nc.vector.tensor_scalar_add(biased[:], products[mb][:], bias[:, mb : mb + 1])
                for q in range(QUEUES):
                    queues[q].dma_start(
                        out[mb * P + q : (mb + 1) * P : QUEUES, first : first + count], biased[q::QUEUES, :]
                    )
